import numpy as np
import ml_dtypes


def mxq(x, axis, fmt="e4m3"):
    dtype, down = {"e4m3": (ml_dtypes.float8_e4m3fn, 7), "e5m2": (ml_dtypes.float8_e5m2, 14)}[fmt]
    v = np.moveaxis(np.asarray(x, np.float32).astype(ml_dtypes.bfloat16).astype(np.float64), axis, -1)
    blocks = v.reshape(v.shape[:-1] + (-1, 32))
    amax = np.abs(blocks).max(-1, keepdims=True)
    byte = np.maximum(np.where(amax > 0, np.frexp(amax)[1] - 1 + 127, 0) - down, 1)
    scale = np.exp2(byte - 127.0)
    codes = (blocks / scale).astype(np.float32).astype(dtype).astype(np.float64)
    return np.moveaxis((codes * scale).reshape(v.shape), -1, axis)


WIDE = False


def mx_kscale(k):
    if not WIDE:
        return np.ones(k)
    levels = np.array([10, -10, 5, -5, 0])
    if k % 512:
        return np.exp2(np.random.permutation(np.resize(levels, k // 32))).repeat(32)
    a = np.empty((k // 512, 16))
    for p in range(k // 512):
        a[p, :8] = np.random.permutation(np.resize(levels, 8))
        for g in range(8):
            far = levels[np.abs(levels - a[p, g]) >= 10]
            a[p, g + 8] = far[np.random.randint(len(far))]
    return np.exp2(a.ravel()).repeat(32)


def f64(x):
    return np.asarray(x).astype(np.float64)


def striped(idx):
    return np.tile(idx.reshape(-1, 16).T, (8, 1)).astype(np.uint16)


def unstriped(offs):
    return offs[:16].T.reshape(-1).astype(np.int64)


def striped8(idx):
    return np.concatenate([x.reshape(-1, 16).T for x in idx]).astype(np.uint16)


def runs(offs, k):
    lists = np.stack([offs[16 * r : 16 * r + 16].T.reshape(-1) for r in range(8)]).astype(np.int64)
    return lists[np.arange(k) % 512 // 64]


def pack_weight(w):
    k, n = w.shape
    w = f64(np.asarray(w, np.float32).astype(ml_dtypes.bfloat16)).reshape(k // 32, 32, n)
    amax = np.abs(w).max(1)
    byte = np.clip(np.where(amax > 0, np.frexp(amax)[1] - 1 + 127 - 7, 1), 1, 254)
    scaled = (w * np.exp2(127.0 - byte)[:, None, :]).reshape(k, n).astype(np.float32)
    words = np.ascontiguousarray(scaled.reshape(k // 512, 128, 4, n).transpose(0, 1, 3, 2)).astype(ml_dtypes.float8_e4m3fn).view(np.uint8)
    return words, np.ascontiguousarray(byte.astype(np.uint8).reshape(k // 512, 16, n))


def unpack_weight(words, scales):
    g, p, n, _ = words.shape
    vals = np.ascontiguousarray(words).view(ml_dtypes.float8_e4m3fn).astype(np.float64) * np.repeat(np.exp2(scales.astype(np.float64) - 127.0), 8, axis=1)[..., None]
    return vals.transpose(0, 1, 3, 2).reshape(g * 512, n)


def relu(v):
    return np.maximum(v, 0.0)


K, T, S, N, H, U = 512, 2048, 512, 512, 512, 1024


def setup_inputs():
    n = np.random.standard_normal
    s = mx_kscale(K)[:, None]
    u = mx_kscale(S)
    packed_xT = pack_weight(n((K, T)) * s)
    return {
        "x_words": packed_xT[0],
        "x_scales": packed_xT[1],
        "wa": (n((K, H)) / np.sqrt(K) / s).astype(np.float32),
        "wb": (n((K, N)) / np.sqrt(K) / s).astype(np.float32),
        "gt": (np.random.uniform(0.5, 1.5, (S, 1)) * u[:, None]).astype(np.float32),
        "gi": (np.random.uniform(0.5, 1.5, (S, 1)) / u[:, None]).astype(np.float32),
        "offs": striped(np.random.permutation(T)[:S]),
        "two": striped(np.random.permutation(T)[:S]),
        "n1": striped8(np.stack([np.random.permutation(H) for _ in range(8)])),
        "n2": striped8(np.stack([np.random.permutation(H) for _ in range(8)])),
        "n3": striped8(np.stack([np.random.permutation(U)[:N] for _ in range(8)])),
        "n4": striped8(np.stack([np.random.permutation(N) for _ in range(8)])),
        "n5": striped8(np.stack([np.random.permutation(U) for _ in range(8)])),
    }


def reference(x_words, x_scales, wa, wb, gt, gi, offs, two, n1, n2, n3, n4, n5):
    xq = unpack_weight(x_words, x_scales)[:, unstriped(offs)]
    a = xq.T @ mxq(f64(wa), 0, "e4m3")
    z = f64(gt) * (0.75 * ((a - (a[np.arange(S)[:, None], runs(n1, S)])) * (a - (a[np.arange(S)[:, None], runs(n2, S)]))))
    x_two = unpack_weight(x_words, x_scales)[:, unstriped(two)]
    b = x_two.T @ mxq(f64(wb), 0, "e4m3")
    nw = b - (relu(b[np.arange(S)[:, None], runs(n4, S)]))
    pg = np.zeros((S, U))
    pg[np.arange(S)[:, None], runs(n3, S)] = nw
    z2 = f64(gi) * pg
    cv = 0.0625 * ((mxq(z, 0, "e4m3").T @ mxq(z2, 0, "e4m3")))
    pa = cv[np.arange(H)[:, None], runs(n5, H)]
    return (2.0 * (cv * pa)) / ((cv) ** 2 + (pa) ** 2 + 0.5)

@@ -1,0 +1,261 @@
+from contextlib import ExitStack
+
+import concourse.mybir as mybir
+from concourse.masks import make_identity
+
+K, T, S, H, N, U = 512, 2048, 512, 512, 512, 1024
+FLOPS = 2 * K * S * H + 2 * K * S * N + 2 * S * H * U
+
+F32 = mybir.dt.float32
+BF16 = mybir.dt.bfloat16
+I32 = mybir.dt.int32
+U32 = mybir.dt.uint32
+U16 = mybir.dt.uint16
+U8 = mybir.dt.uint8
+FP8X4 = mybir.dt.float8_e4m3fn_x4
+ALU = mybir.AluOpType
+ACT = mybir.ActivationFunctionType
+
+P = 128
+PACK = 4
+BANK = 512
+
+
+def tile_picked_mombquadpagezharm_none_p_kernel(
+    tc, x_words, x_scales, wa, wb, gt, gi, offs, two, n1, n2, n3, n4, n5, out
+):
+    nc = tc.nc
+    with ExitStack() as ctx:
+        keep = ctx.enter_context(tc.tile_pool(name="keep", bufs=1))
+        ring = ctx.enter_context(tc.tile_pool(name="ring", bufs=3))
+        psum = ctx.enter_context(tc.psum_pool(name="psum", bufs=8))
+
+        def load_list(src, name):
+            tile = keep.tile(list(src.shape), U16, name=name)
+            nc.sync.dma_start(tile[:], src)
+            return tile
+
+        def load_weight(w, name):
+            halves = []
+            for h in range(2):
+                raw = keep.tile([P, PACK, 256], F32, name=f"{name}_raw{h}")
+                nc.sync.dma_start(raw[:], w[:, 256 * h : 256 * (h + 1)].rearrange("(p j) n -> p j n", j=PACK))
+                halves.append(raw)
+            return halves
+
+        table_scales = keep.tile([P, T], U8, name="table_scales", align_bytes=64)
+        nc.vector.memset(table_scales[:].bitcast(I32), 0)
+        two_l = load_list(two, "two_l")
+        for q in range(4):
+            nc.sync.dma_start(
+                table_scales[32 * q : 32 * q + 4, :].bitcast(I32), x_scales[0, 4 * q : 4 * q + 4, :].bitcast(I32)
+            )
+        wb_raw = load_weight(wb, "wb")
+        offs_l = load_list(offs, "offs_l")
+        table_words = keep.tile([P, T], I32, name="table_words", align_bytes=64)
+        nc.sync.dma_start(table_words[:], x_words[0].rearrange("p c r -> p (c r)").bitcast(I32))
+        n4_l = load_list(n4, "n4_l")
+        n3_l = load_list(n3, "n3_l")
+        wa_raw = load_weight(wa, "wa")
+        n1_l = load_list(n1, "n1_l")
+        n2_l = load_list(n2, "n2_l")
+        n5_l = load_list(n5, "n5_l")
+
+        gates_rows = keep.tile([P, P], F32, name="gates_rows")
+        nc.gpsimd.memset(gates_rows[:], 0.0)
+        for row, g in ((0, gt), (PACK, gi)):
+            nc.scalar.dma_start(
+                gates_rows[row : row + PACK, :].rearrange("t (g r) -> t g r", r=8),
+                g.rearrange("(g t r) o -> t g (r o)", t=PACK, r=8),
+            )
+        ident = keep.tile([P, P], F32, name="ident")
+        make_identity(nc, ident[:])
+        gates_bank = psum.tile([P, BANK], F32, name="bank")
+        nc.tensor.transpose(gates_bank[:, :P], gates_rows[:], ident[:])
+        gates = keep.tile([P, 2 * PACK], F32, name="gates")
+        nc.scalar.copy(gates[:], gates_bank[:, : 2 * PACK])
+        gt_c, gi_c = gates[:, :PACK], gates[:, PACK:]
+        half_sign = keep.tile([P, PACK], F32, name="half_sign")
+        nc.gpsimd.tensor_scalar(half_sign[:], gi_c, 0.0, 0.5, ALU.is_lt, ALU.subtract)
+        half_mag = keep.tile([P, PACK], F32, name="half_mag")
+        nc.gpsimd.tensor_tensor(half_mag[:], half_sign[:], gi_c, ALU.mult)
+        gi_mag = keep.tile([P, PACK], F32, name="gi_mag")
+        nc.gpsimd.tensor_scalar(gi_mag[:], half_mag[:], -2.0, 0.0, ALU.mult, ALU.add)
+        gi_neg = keep.tile([P, PACK], F32, name="gi_neg")
+        nc.gpsimd.tensor_scalar(gi_neg[:], half_mag[:], 2.0, 0.0, ALU.mult, ALU.add)
+        half_gt = keep.tile([P, PACK], F32, name="half_gt")
+        nc.gpsimd.tensor_tensor(half_gt[:], half_sign[:], gt_c, ALU.mult)
+        a_scale = keep.tile([P, PACK], F32, name="a_scale")
+        nc.gpsimd.tensor_scalar(a_scale[:], half_gt[:], 1.5, 0.0, ALU.mult, ALU.add)
+
+        pages = [keep.tile([P, U], F32, name=f"page{t}") for t in range(PACK)]
+        for page in pages:
+            nc.vector.memset(page[:], 0.0)
+
+        def pick_words(lst, name):
+            words = keep.tile([P, S], U32, name=f"{name}_words", align_bytes=64)
+            nc.vector.tensor_copy(
+                words[:].rearrange("p (t g r) -> p g t r", t=PACK, r=8), table_words[:].bitcast(U32).indirect(lst[:])
+            )
+            return words
+
+        def pick_scales(lst, name):
+            picked = keep.tile([P, S], U8, name=f"{name}_picked", align_bytes=64)
+            nc.vector.tensor_copy(picked[:], table_scales[:].indirect(lst[:]))
+            scales = keep.tile([P, S], U8, name=f"{name}_scales", align_bytes=64)
+            nc.vector.tensor_copy(
+                scales[:].bitcast(I32).rearrange("p (t g r) -> p g t r", t=PACK, r=2),
+                picked[:].bitcast(I32).rearrange("p (g t r) -> p g t r", t=PACK, r=2),
+            )
+            return scales
+
+        def interleave(dst, src):
+            nc.scalar.copy(
+                dst.rearrange("p (c i) t -> p c t i", i=4),
+                src.rearrange("p t (c i) -> p c t i", i=4),
+            )
+
+        def quantize_weight(halves, name):
+            grouped = keep.tile([P, BANK, PACK], BF16, name=f"{name}_grouped", align_bytes=64)
+            codes = keep.tile([P, BANK], U32, name=f"{name}_codes", align_bytes=64)
+            scales = keep.tile([P, BANK], U8, name=f"{name}_plane", align_bytes=64)
+            for h, raw in enumerate(halves):
+                cols = slice(256 * h, 256 * (h + 1))
+                interleave(grouped[:, cols, :], raw[:])
+                nc.vector.quantize_mx(
+                    codes[:, cols].bitcast(FP8X4), scales[:, cols], grouped[:, cols, :].rearrange("p n j -> p (n j)")
+                )
+            return codes, scales
+
+        def product(lhs, t, rhs, cols):
+            bank = psum.tile([P, BANK], F32, name="bank")
+            rows = slice(P * t, P * (t + 1))
+            nc.tensor.matmul_mx(
+                bank[:],
+                lhsT=lhs[0][:, rows].bitcast(FP8X4),
+                lhsT_scale=lhs[1][:, rows],
+                rhs=rhs[0][:, cols].bitcast(FP8X4),
+                rhs_scale=rhs[1][:, cols],
+                start=True,
+                stop=True,
+            )
+            return bank
+
+        scales_b = pick_scales(two_l, "b")
+        scales_a = pick_scales(offs_l, "a")
+        wb_q = quantize_weight(wb_raw, "wb")
+        tokens_b = (pick_words(two_l, "b"), scales_b)
+        tokens_a = (pick_words(offs_l, "a"), scales_a)
+
+        b_rows = []
+        for t in range(PACK):
+            bank = product(tokens_b, t, wb_q, slice(0, N))
+            rows = keep.tile([P, 2 * N], F32, name=f"b_rows{t}")
+            nc.scalar.activation(rows[:, :N], bank[:], ACT.Relu, scale=gi_mag[:, t : t + 1])
+            nc.scalar.activation(rows[:, N:], bank[:], ACT.Copy, scale=gi_neg[:, t : t + 1])
+            b_rows.append(rows)
+
+        wa_q = quantize_weight(wa_raw, "wa")
+        a_rows = []
+        for t in range(PACK):
+            bank = product(tokens_a, t, wa_q, slice(0, H))
+            first = keep.tile([P, 2 * H], F32, name=f"a_first{t}")
+            second = keep.tile([P, 2 * H], F32, name=f"a_second{t}")
+            nc.scalar.copy(first[:, :H], bank[:])
+            nc.scalar.activation(first[:, H:], bank[:], ACT.Copy, scale=a_scale[:, t : t + 1])
+            nc.scalar.activation(second[:, :H], bank[:], ACT.Copy, scale=a_scale[:, t : t + 1])
+            nc.scalar.copy(second[:, H:], bank[:])
+            a_rows.append((first, second))
+
+        z2_planes = keep.tile([P, PACK, U], BF16, name="z2_planes")
+        fetched = []
+        for t in range(PACK + 1):
+            if t < PACK:
+                got = ring.tile([P, N], F32, name="b_fetched")
+                nc.vector.tensor_copy(got[:], b_rows[t][:].indirect(n4_l[:]))
+                fetched.append(got)
+            if t > 0:
+                s = t - 1
+                nc.vector.tensor_tensor(pages[s][:].indirect(n3_l[:]), fetched[s][:], b_rows[s][:, N:], ALU.add)
+                nc.scalar.copy(z2_planes[:, s, :], pages[s][:])
+
+        z2_grouped = keep.tile([P, U, PACK], BF16, name="z2_grouped", align_bytes=64)
+        z2_codes = keep.tile([P, U], U32, name="z2_codes", align_bytes=64)
+        z2_scales = keep.tile([P, U], U8, name="z2_scales", align_bytes=64)
+        for h in range(2):
+            cols = slice(BANK * h, BANK * (h + 1))
+            interleave(z2_grouped[:, cols, :], z2_planes[:, :, cols])
+
+        d1 = keep.tile([P, PACK, H], F32, name="d1")
+        d2 = keep.tile([P, PACK, H], F32, name="d2")
+        for t in range(PACK):
+            first, second = a_rows[t]
+            nc.vector.tensor_tensor(d1[:, t, :], first[:].indirect(n1_l[:]), second[:, H:], ALU.subtract)
+            nc.vector.tensor_tensor(d2[:, t, :], second[:].indirect(n2_l[:]), first[:, H:], ALU.subtract)
+        for h in range(2):
+            cols = slice(BANK * h, BANK * (h + 1))
+            nc.vector.quantize_mx(
+                z2_codes[:, cols].bitcast(FP8X4), z2_scales[:, cols], z2_grouped[:, cols, :].rearrange("p n j -> p (n j)")
+            )
+        z_grouped = keep.tile([P, PACK, P, PACK], BF16, name="z_grouped", align_bytes=64)
+        nc.vector.tensor_tensor(
+            z_grouped[:].rearrange("p f m t -> p m t f"),
+            d1[:].rearrange("p t (m f) -> p m t f", f=PACK),
+            d2[:].rearrange("p t (m f) -> p m t f", f=PACK),
+            ALU.mult,
+        )
+        z_codes = keep.tile([P, H], U32, name="z_codes", align_bytes=64)
+        z_scales = keep.tile([P, H], U8, name="z_scales", align_bytes=64)
+        for f in range(PACK):
+            rows = slice(P * f, P * (f + 1))
+            nc.vector.quantize_mx(
+                z_codes[:, rows].bitcast(FP8X4), z_scales[:, rows], z_grouped[:, f].rearrange("p m t -> p (m t)")
+            )
+
+        out_rows = out.rearrange("(m f) w -> f m w", f=PACK)
+        units = 2 * PACK
+        cvs = [keep.tile([P, U], F32, name=f"cv{f}") for f in range(PACK)]
+        held = {}
+
+        def cols_of(u):
+            return slice(BANK * (u % 2), BANK * (u % 2 + 1))
+
+        def new(name, u):
+            held[name, u] = ring.tile([P, BANK], F32, name=name)
+            return held[name, u][:]
+
+        def moments(u):
+            bank = product((z_codes, z_scales), u // 2, (z2_codes, z2_scales), cols_of(u))
+            nc.scalar.activation(cvs[u // 2][:, cols_of(u)], bank[:], ACT.Copy, scale=0.0625)
+
+        def fetch(u):
+            nc.vector.tensor_copy(new("pa", u), cvs[u // 2][:].indirect(n5_l[:, 32 * (u % 2) : 32 * (u % 2 + 1)]))
+
+        def square_cv(u):
+            nc.scalar.activation(new("cv_sq", u), cvs[u // 2][:, cols_of(u)], ACT.Square)
+
+        def square_pa(u):
+            nc.scalar.activation(new("pa_sq", u), held["pa", u][:], ACT.Square)
+
+        def numerator(u):
+            nc.vector.scalar_tensor_tensor(new("num", u), cvs[u // 2][:, cols_of(u)], 2.0, held["pa", u][:], ALU.mult, ALU.mult)
+
+        def denominator(u):
+            nc.vector.scalar_tensor_tensor(new("den", u), held["cv_sq", u][:], 0.5, held["pa_sq", u][:], ALU.add, ALU.add)
+
+        def root(u):
+            nc.scalar.activation(new("root", u), held["den", u][:], ACT.Abs_reciprocal_sqrt)
+
+        def inverse(u):
+            nc.scalar.activation(new("inv", u), held["root", u][:], ACT.Square)
+
+        def finish(u):
+            res = new("res", u)
+            nc.vector.tensor_tensor(res, held["num", u][:], held["inv", u][:], ALU.mult)
+            nc.sync.dma_start(out_rows[u // 2][:, cols_of(u)], res)
+
+        stages = ((fetch, 1), (moments, 3), (inverse, -1), (denominator, 0), (square_pa, 1), (numerator, 0), (root, 0), (finish, -1), (square_cv, 2))
+        for step in range(-3, units + 1):
+            for stage, ahead in stages:
+                if 0 <= step + ahead < units:
+                    stage(step + ahead)

@@ -35,62 +35,56 @@ def tile_picked_mombquadpagezharm_none_p_kernel(
             nc.sync.dma_start(tile[:], src)
             return tile
 
-        def load_weight(w, name):
-            halves = []
-            for h in range(2):
-                raw = keep.tile([P, PACK, 256], F32, name=f"{name}_raw{h}")
-                nc.sync.dma_start(raw[:], w[:, 256 * h : 256 * (h + 1)].rearrange("(p j) n -> p j n", j=PACK))
-                halves.append(raw)
-            return halves
+        def load_weight(w, name, h):
+            raw = keep.tile([P, PACK, 256], F32, name=f"{name}_raw{h}", tag=f"{name}_raw{h}")
+            nc.sync.dma_start(raw[:], w[:, 256 * h : 256 * (h + 1)].rearrange("(p j) n -> p j n", j=PACK))
+            return raw
 
         table_scales = keep.tile([P, T], U8, name="table_scales", align_bytes=64)
-        nc.vector.memset(table_scales[:].bitcast(I32), 0)
+        nc.gpsimd.memset(table_scales[:].bitcast(I32), 0)
         two_l = load_list(two, "two_l")
+        offs_l = load_list(offs, "offs_l")
         for q in range(4):
             nc.sync.dma_start(
                 table_scales[32 * q : 32 * q + 4, :].bitcast(I32), x_scales[0, 4 * q : 4 * q + 4, :].bitcast(I32)
             )
-        wb_raw = load_weight(wb, "wb")
-        offs_l = load_list(offs, "offs_l")
+        wb_raw = [load_weight(wb, "wb", h) for h in range(2)]
         table_words = keep.tile([P, T], I32, name="table_words", align_bytes=64)
         nc.sync.dma_start(table_words[:], x_words[0].rearrange("p c r -> p (c r)").bitcast(I32))
+        gates_rows = keep.tile([P, P], F32, name="gates_rows")
+        nc.vector.memset(gates_rows[:], 0.0)
+        for row, g in ((0, gt), (PACK, gi)):
+            nc.sync.dma_start(
+                gates_rows[row : row + PACK, :].rearrange("t (g r) -> t g r", r=8),
+                g.rearrange("(g t r) o -> t g (r o)", t=PACK, r=8),
+            )
         n4_l = load_list(n4, "n4_l")
         n3_l = load_list(n3, "n3_l")
-        wa_raw = load_weight(wa, "wa")
+        wa_raw = [load_weight(wa, "wa", h) for h in range(2)]
         n1_l = load_list(n1, "n1_l")
         n2_l = load_list(n2, "n2_l")
         n5_l = load_list(n5, "n5_l")
 
-        gates_rows = keep.tile([P, P], F32, name="gates_rows")
-        nc.gpsimd.memset(gates_rows[:], 0.0)
-        for row, g in ((0, gt), (PACK, gi)):
-            nc.scalar.dma_start(
-                gates_rows[row : row + PACK, :].rearrange("t (g r) -> t g r", r=8),
-                g.rearrange("(g t r) o -> t g (r o)", t=PACK, r=8),
-            )
+        warm = keep.tile([P, 2], F32, name="warm")
+        nc.vector.memset(warm[:, 0:1], 1.0)
+        nc.scalar.activation(warm[:, 1:2], warm[:, 0:1], ACT.Abs_reciprocal_sqrt)
+
         ident = keep.tile([P, P], F32, name="ident")
         make_identity(nc, ident[:])
         gates_bank = psum.tile([P, BANK], F32, name="bank")
         nc.tensor.transpose(gates_bank[:, :P], gates_rows[:], ident[:])
-        gates = keep.tile([P, 2 * PACK], F32, name="gates")
-        nc.scalar.copy(gates[:], gates_bank[:, : 2 * PACK])
-        gt_c, gi_c = gates[:, :PACK], gates[:, PACK:]
+        gt_c, gi_c = gates_bank[:, :PACK], gates_bank[:, PACK : 2 * PACK]
         half_sign = keep.tile([P, PACK], F32, name="half_sign")
-        nc.gpsimd.tensor_scalar(half_sign[:], gi_c, 0.0, 0.5, ALU.is_lt, ALU.subtract)
-        half_mag = keep.tile([P, PACK], F32, name="half_mag")
-        nc.gpsimd.tensor_tensor(half_mag[:], half_sign[:], gi_c, ALU.mult)
+        nc.vector.tensor_scalar(half_sign[:], gi_c, 0.0, 0.5, ALU.is_lt, ALU.subtract)
         gi_mag = keep.tile([P, PACK], F32, name="gi_mag")
-        nc.gpsimd.tensor_scalar(gi_mag[:], half_mag[:], -2.0, 0.0, ALU.mult, ALU.add)
         gi_neg = keep.tile([P, PACK], F32, name="gi_neg")
-        nc.gpsimd.tensor_scalar(gi_neg[:], half_mag[:], 2.0, 0.0, ALU.mult, ALU.add)
-        half_gt = keep.tile([P, PACK], F32, name="half_gt")
-        nc.gpsimd.tensor_tensor(half_gt[:], half_sign[:], gt_c, ALU.mult)
         a_scale = keep.tile([P, PACK], F32, name="a_scale")
-        nc.gpsimd.tensor_scalar(a_scale[:], half_gt[:], 1.5, 0.0, ALU.mult, ALU.add)
+        for dst, factor, gate in ((gi_mag, -2.0, gi_c), (gi_neg, 2.0, gi_c), (a_scale, 1.5, gt_c)):
+            nc.vector.scalar_tensor_tensor(dst[:], half_sign[:], factor, gate, ALU.mult, ALU.mult)
 
         pages = [keep.tile([P, U], F32, name=f"page{t}") for t in range(PACK)]
         for page in pages:
-            nc.vector.memset(page[:], 0.0)
+            nc.gpsimd.memset(page[:], 0.0)
 
         def pick_words(lst, name):
             words = keep.tile([P, S], U32, name=f"{name}_words", align_bytes=64)
@@ -116,7 +110,7 @@ def tile_picked_mombquadpagezharm_none_p_kernel(
             )
 
         def quantize_weight(halves, name):
-            grouped = keep.tile([P, BANK, PACK], BF16, name=f"{name}_grouped", align_bytes=64)
+            grouped = keep.tile([P, BANK, PACK], BF16, name=f"{name}_grouped", tag=f"{name}_grouped", align_bytes=64)
             codes = keep.tile([P, BANK], U32, name=f"{name}_codes", align_bytes=64)
             scales = keep.tile([P, BANK], U8, name=f"{name}_plane", align_bytes=64)
             for h, raw in enumerate(halves):
@@ -151,9 +145,10 @@ def tile_picked_mombquadpagezharm_none_p_kernel(
         for t in range(PACK):
             bank = product(tokens_b, t, wb_q, slice(0, N))
             rows = keep.tile([P, 2 * N], F32, name=f"b_rows{t}")
+            neg = keep.tile([P, N], F32, name=f"b_neg{t}")
             nc.scalar.activation(rows[:, :N], bank[:], ACT.Relu, scale=gi_mag[:, t : t + 1])
-            nc.scalar.activation(rows[:, N:], bank[:], ACT.Copy, scale=gi_neg[:, t : t + 1])
-            b_rows.append(rows)
+            nc.scalar.activation(neg[:], bank[:], ACT.Copy, scale=gi_neg[:, t : t + 1])
+            b_rows.append((rows, neg))
 
         wa_q = quantize_weight(wa_raw, "wa")
         a_rows = []
@@ -162,21 +157,20 @@ def tile_picked_mombquadpagezharm_none_p_kernel(
             first = keep.tile([P, 2 * H], F32, name=f"a_first{t}")
             second = keep.tile([P, 2 * H], F32, name=f"a_second{t}")
             nc.scalar.copy(first[:, :H], bank[:])
-            nc.scalar.activation(first[:, H:], bank[:], ACT.Copy, scale=a_scale[:, t : t + 1])
             nc.scalar.activation(second[:, :H], bank[:], ACT.Copy, scale=a_scale[:, t : t + 1])
-            nc.scalar.copy(second[:, H:], bank[:])
+            nc.scalar.activation(first[:, H:], bank[:], ACT.Copy, scale=a_scale[:, t : t + 1])
             a_rows.append((first, second))
 
-        z2_planes = keep.tile([P, PACK, U], BF16, name="z2_planes")
-        fetched = []
+        z2_planes = keep.tile([P, PACK, U], BF16, name="z2_planes", tag="wa_raw1")
+        early = keep.tile([P, 2, N], F32, name="b_fetched_early")
+        late = keep.tile([P, 2, N], F32, name="b_fetched_late", tag="wa_grouped", align_bytes=64)
+        fetched = [early[:, 0, :], early[:, 1, :], late[:, 0, :], late[:, 1, :]]
         for t in range(PACK + 1):
             if t < PACK:
-                got = ring.tile([P, N], F32, name="b_fetched")
-                nc.vector.tensor_copy(got[:], b_rows[t][:].indirect(n4_l[:]))
-                fetched.append(got)
+                nc.vector.tensor_copy(fetched[t], b_rows[t][0][:].indirect(n4_l[:]))
             if t > 0:
                 s = t - 1
-                nc.vector.tensor_tensor(pages[s][:].indirect(n3_l[:]), fetched[s][:], b_rows[s][:, N:], ALU.add)
+                nc.vector.tensor_tensor(pages[s][:].indirect(n3_l[:]), fetched[s], b_rows[s][1][:], ALU.add)
                 nc.scalar.copy(z2_planes[:, s, :], pages[s][:])
 
         z2_grouped = keep.tile([P, U, PACK], BF16, name="z2_grouped", align_bytes=64)
@@ -186,22 +180,28 @@ def tile_picked_mombquadpagezharm_none_p_kernel(
             cols = slice(BANK * h, BANK * (h + 1))
             interleave(z2_grouped[:, cols, :], z2_planes[:, :, cols])
 
-        d1 = keep.tile([P, PACK, H], F32, name="d1")
-        d2 = keep.tile([P, PACK, H], F32, name="d2")
+        diffs = keep.tile([P, PACK, 2 * H], F32, name="diffs")
         for t in range(PACK):
             first, second = a_rows[t]
-            nc.vector.tensor_tensor(d1[:, t, :], first[:].indirect(n1_l[:]), second[:, H:], ALU.subtract)
-            nc.vector.tensor_tensor(d2[:, t, :], second[:].indirect(n2_l[:]), first[:, H:], ALU.subtract)
-        for h in range(2):
-            cols = slice(BANK * h, BANK * (h + 1))
-            nc.vector.quantize_mx(
-                z2_codes[:, cols].bitcast(FP8X4), z2_scales[:, cols], z2_grouped[:, cols, :].rearrange("p n j -> p (n j)")
-            )
+            got = ring.tile([P, 2 * H], F32, name="a_fetched", bufs=2)
+            nc.vector.tensor_copy(got[:, :H], first[:].indirect(n1_l[:]))
+            nc.vector.tensor_copy(got[:, H:], second[:].indirect(n2_l[:]))
+            if t < PACK - 1:
+                nc.gpsimd.tensor_tensor(diffs[:, t, :], got[:], first[:], ALU.subtract)
+            else:
+                for h in range(2):
+                    cols = slice(BANK * h, BANK * (h + 1))
+                    nc.vector.quantize_mx(
+                        z2_codes[:, cols].bitcast(FP8X4),
+                        z2_scales[:, cols],
+                        z2_grouped[:, cols, :].rearrange("p n j -> p (n j)"),
+                    )
+                nc.vector.tensor_tensor(diffs[:, t, :], got[:], first[:], ALU.subtract)
         z_grouped = keep.tile([P, PACK, P, PACK], BF16, name="z_grouped", align_bytes=64)
         nc.vector.tensor_tensor(
             z_grouped[:].rearrange("p f m t -> p m t f"),
-            d1[:].rearrange("p t (m f) -> p m t f", f=PACK),
-            d2[:].rearrange("p t (m f) -> p m t f", f=PACK),
+            diffs[:, :, :H].rearrange("p t (m f) -> p m t f", f=PACK),
+            diffs[:, :, H:].rearrange("p t (m f) -> p m t f", f=PACK),
             ALU.mult,
         )
         z_codes = keep.tile([P, H], U32, name="z_codes", align_bytes=64)
@@ -214,48 +214,66 @@ def tile_picked_mombquadpagezharm_none_p_kernel(
 
         out_rows = out.rearrange("(m f) w -> f m w", f=PACK)
         units = 2 * PACK
-        cvs = [keep.tile([P, U], F32, name=f"cv{f}") for f in range(PACK)]
+        cvs = [keep.tile([P, U], F32, name=f"cv{f}", tag=f"b_rows{f}") for f in range(PACK)]
         held = {}
+        shared = units - 2
 
         def cols_of(u):
             return slice(BANK * (u % 2), BANK * (u % 2 + 1))
 
-        def new(name, u):
-            held[name, u] = ring.tile([P, BANK], F32, name=name)
+        def new(name, u, bufs=2):
+            held[name, u] = ring.tile([P, BANK], F32, name=name, bufs=bufs)
             return held[name, u][:]
 
         def moments(u):
-            bank = product((z_codes, z_scales), u // 2, (z2_codes, z2_scales), cols_of(u))
-            nc.scalar.activation(cvs[u // 2][:, cols_of(u)], bank[:], ACT.Copy, scale=0.0625)
+            held["bank", u] = product((z_codes, z_scales), u // 2, (z2_codes, z2_scales), cols_of(u))
+            nc.scalar.activation(cvs[u // 2][:, cols_of(u)], held["bank", u][:], ACT.Copy, scale=0.0625)
 
         def fetch(u):
-            nc.vector.tensor_copy(new("pa", u), cvs[u // 2][:].indirect(n5_l[:, 32 * (u % 2) : 32 * (u % 2 + 1)]))
+            nc.vector.tensor_copy(new("pa", u, 4), cvs[u // 2][:].indirect(n5_l[:, 32 * (u % 2) : 32 * (u % 2 + 1)]))
 
         def square_cv(u):
-            nc.scalar.activation(new("cv_sq", u), cvs[u // 2][:, cols_of(u)], ACT.Square)
+            if u >= shared:
+                nc.scalar.activation(new("cv_sq", u), cvs[u // 2][:, cols_of(u)], ACT.Square)
+                return
+            nc.vector.scalar_tensor_tensor(
+                new("cv_sq", u), held["bank", u][:], 0.0625, cvs[u // 2][:, cols_of(u)], ALU.mult, ALU.mult
+            )
 
         def square_pa(u):
             nc.scalar.activation(new("pa_sq", u), held["pa", u][:], ACT.Square)
 
-        def numerator(u):
-            nc.vector.scalar_tensor_tensor(new("num", u), cvs[u // 2][:, cols_of(u)], 2.0, held["pa", u][:], ALU.mult, ALU.mult)
-
         def denominator(u):
-            nc.vector.scalar_tensor_tensor(new("den", u), held["cv_sq", u][:], 0.5, held["pa_sq", u][:], ALU.add, ALU.add)
+            engine = nc.gpsimd if u < shared else nc.vector
+            engine.tensor_tensor(new("den", u), held["cv_sq", u][:], held["pa_sq", u][:], ALU.add)
 
         def root(u):
-            nc.scalar.activation(new("root", u), held["den", u][:], ACT.Abs_reciprocal_sqrt)
+            nc.scalar.activation(new("root", u), held["den", u][:], ACT.Abs_reciprocal_sqrt, bias=0.5)
 
         def inverse(u):
             nc.scalar.activation(new("inv", u), held["root", u][:], ACT.Square)
 
+        def ratio(u):
+            if u < shared:
+                nc.gpsimd.tensor_tensor(new("ratio", u), held["pa", u][:], held["inv", u][:], ALU.mult)
+
+        def numerator(u):
+            if u >= shared:
+                nc.vector.scalar_tensor_tensor(new("num", u), held["bank", u][:], 0.125, held["pa", u][:], ALU.mult, ALU.mult)
+
         def finish(u):
-            res = new("res", u)
-            nc.vector.tensor_tensor(res, held["num", u][:], held["inv", u][:], ALU.mult)
+            res = new("res", u, 3)
+            if u < shared:
+                nc.vector.scalar_tensor_tensor(res, held["bank", u][:], 0.125, held["ratio", u][:], ALU.mult, ALU.mult)
+            else:
+                nc.vector.tensor_tensor(res, held["num", u][:], held["inv", u][:], ALU.mult)
             nc.sync.dma_start(out_rows[u // 2][:, cols_of(u)], res)
 
-        stages = ((fetch, 1), (moments, 3), (inverse, -1), (denominator, 0), (square_pa, 1), (numerator, 0), (root, 0), (finish, -1), (square_cv, 2))
-        for step in range(-3, units + 1):
+        stages = (
+            (fetch, 1), (denominator, 0), (inverse, -1), (moments, 3), (square_cv, 1), (square_pa, 1), (ratio, -1),
+            (root, 0), (numerator, 0), (finish, -2),
+        )
+        for step in range(-3, units + 2):
             for stage, ahead in stages:
                 if 0 <= step + ahead < units:
                     stage(step + ahead)

@@ -28,7 +28,7 @@ def tile_picked_mombquadpagezharm_none_p_kernel(
     with ExitStack() as ctx:
         keep = ctx.enter_context(tc.tile_pool(name="keep", bufs=1))
         ring = ctx.enter_context(tc.tile_pool(name="ring", bufs=3))
-        psum = ctx.enter_context(tc.psum_pool(name="psum", bufs=8))
+        psum = ctx.enter_context(tc.psum_pool(name="psum", bufs=4))
 
         def load_list(src, name):
             tile = keep.tile(list(src.shape), U16, name=name)
@@ -49,8 +49,6 @@ def tile_picked_mombquadpagezharm_none_p_kernel(
                 table_scales[32 * q : 32 * q + 4, :].bitcast(I32), x_scales[0, 4 * q : 4 * q + 4, :].bitcast(I32)
             )
         wb_raw = [load_weight(wb, "wb", h) for h in range(2)]
-        table_words = keep.tile([P, T], I32, name="table_words", align_bytes=64)
-        nc.sync.dma_start(table_words[:], x_words[0].rearrange("p c r -> p (c r)").bitcast(I32))
         gates_rows = keep.tile([P, P], F32, name="gates_rows")
         nc.vector.memset(gates_rows[:], 0.0)
         for row, g in ((0, gt), (PACK, gi)):
@@ -58,6 +56,8 @@ def tile_picked_mombquadpagezharm_none_p_kernel(
                 gates_rows[row : row + PACK, :].rearrange("t (g r) -> t g r", r=8),
                 g.rearrange("(g t r) o -> t g (r o)", t=PACK, r=8),
             )
+        table_words = keep.tile([P, T], I32, name="table_words", align_bytes=64)
+        nc.sync.dma_start(table_words[:], x_words[0].rearrange("p c r -> p (c r)").bitcast(I32))
         n4_l = load_list(n4, "n4_l")
         n3_l = load_list(n3, "n3_l")
         wa_raw = [load_weight(wa, "wa", h) for h in range(2)]
@@ -183,7 +183,7 @@ def tile_picked_mombquadpagezharm_none_p_kernel(
         diffs = keep.tile([P, PACK, 2 * H], F32, name="diffs")
         for t in range(PACK):
             first, second = a_rows[t]
-            got = ring.tile([P, 2 * H], F32, name="a_fetched", bufs=2)
+            got = ring.tile([P, 2 * H], F32, name="a_fetched", bufs=3)
             nc.vector.tensor_copy(got[:, :H], first[:].indirect(n1_l[:]))
             nc.vector.tensor_copy(got[:, H:], second[:].indirect(n2_l[:]))
             if t < PACK - 1:
@@ -198,25 +198,27 @@ def tile_picked_mombquadpagezharm_none_p_kernel(
                     )
                 nc.vector.tensor_tensor(diffs[:, t, :], got[:], first[:], ALU.subtract)
         z_grouped = keep.tile([P, PACK, P, PACK], BF16, name="z_grouped", align_bytes=64)
-        nc.vector.tensor_tensor(
-            z_grouped[:].rearrange("p f m t -> p m t f"),
-            diffs[:, :, :H].rearrange("p t (m f) -> p m t f", f=PACK),
-            diffs[:, :, H:].rearrange("p t (m f) -> p m t f", f=PACK),
-            ALU.mult,
-        )
         z_codes = keep.tile([P, H], U32, name="z_codes", align_bytes=64)
         z_scales = keep.tile([P, H], U8, name="z_scales", align_bytes=64)
-        for f in range(PACK):
-            rows = slice(P * f, P * (f + 1))
-            nc.vector.quantize_mx(
-                z_codes[:, rows].bitcast(FP8X4), z_scales[:, rows], z_grouped[:, f].rearrange("p m t -> p (m t)")
-            )
+        d1 = diffs[:, :, :H].rearrange("p t (a f i) -> p f a t i", f=PACK, i=4)
+        d2 = diffs[:, :, H:].rearrange("p t (a f i) -> p f a t i", f=PACK, i=4)
+        for f in range(PACK + 1):
+            if f < PACK:
+                nc.vector.tensor_tensor(
+                    z_grouped[:, f].rearrange("p (a i) t -> p a t i", i=4), d1[:, f], d2[:, f], ALU.mult
+                )
+            if f > 0:
+                rows = slice(P * (f - 1), P * f)
+                nc.vector.quantize_mx(
+                    z_codes[:, rows].bitcast(FP8X4), z_scales[:, rows], z_grouped[:, f - 1].rearrange("p m t -> p (m t)")
+                )
 
-        out_rows = out.rearrange("(m f) w -> f m w", f=PACK)
+        out_rows = out.rearrange("(a f i) w -> f a i w", f=PACK, i=4)
         units = 2 * PACK
         cvs = [keep.tile([P, U], F32, name=f"cv{f}", tag=f"b_rows{f}") for f in range(PACK)]
         held = {}
-        shared = units - 2
+        turned_units = units - 2
+        blocks = [slice(P * j, P * (j + 1)) for j in range(BANK // P)]
 
         def cols_of(u):
             return slice(BANK * (u % 2), BANK * (u % 2 + 1))
@@ -226,54 +228,76 @@ def tile_picked_mombquadpagezharm_none_p_kernel(
             return held[name, u][:]
 
         def moments(u):
-            held["bank", u] = product((z_codes, z_scales), u // 2, (z2_codes, z2_scales), cols_of(u))
-            nc.scalar.activation(cvs[u // 2][:, cols_of(u)], held["bank", u][:], ACT.Copy, scale=0.0625)
+            bank = product((z_codes, z_scales), u // 2, (z2_codes, z2_scales), cols_of(u))
+            cv = cvs[u // 2]
+            if u == 1:
+                nc.vector.tensor_scalar(cv[:, cols_of(u)], bank[:], 0.0625, None, ALU.mult)
+            else:
+                nc.scalar.activation(cv[:, cols_of(u)], bank[:], ACT.Copy, scale=0.0625)
+            if u in (3, 5):
+                both = ring.tile([P, U], F32, name="cv_sq_row", bufs=2)
+                nc.gpsimd.tensor_tensor(both[:], cv[:], cv[:], ALU.mult)
+                held["cv_sq", u - 1], held["cv_sq", u] = both[:, :BANK], both[:, BANK:]
 
         def fetch(u):
             nc.vector.tensor_copy(new("pa", u, 4), cvs[u // 2][:].indirect(n5_l[:, 32 * (u % 2) : 32 * (u % 2 + 1)]))
 
         def square_cv(u):
-            if u >= shared:
+            if ("cv_sq", u) not in held:
                 nc.scalar.activation(new("cv_sq", u), cvs[u // 2][:, cols_of(u)], ACT.Square)
-                return
-            nc.vector.scalar_tensor_tensor(
-                new("cv_sq", u), held["bank", u][:], 0.0625, cvs[u // 2][:, cols_of(u)], ALU.mult, ALU.mult
-            )
 
         def square_pa(u):
-            nc.scalar.activation(new("pa_sq", u), held["pa", u][:], ACT.Square)
-
-        def denominator(u):
-            engine = nc.gpsimd if u < shared else nc.vector
-            engine.tensor_tensor(new("den", u), held["cv_sq", u][:], held["pa_sq", u][:], ALU.add)
-
-        def root(u):
-            nc.scalar.activation(new("root", u), held["den", u][:], ACT.Abs_reciprocal_sqrt, bias=0.5)
-
-        def inverse(u):
-            nc.scalar.activation(new("inv", u), held["root", u][:], ACT.Square)
-
-        def ratio(u):
-            if u < shared:
-                nc.gpsimd.tensor_tensor(new("ratio", u), held["pa", u][:], held["inv", u][:], ALU.mult)
+            nc.scalar.activation(new("pa_sq", u, 3), held["pa", u][:], ACT.Square)
 
         def numerator(u):
-            if u >= shared:
-                nc.vector.scalar_tensor_tensor(new("num", u), held["bank", u][:], 0.125, held["pa", u][:], ALU.mult, ALU.mult)
+            nc.gpsimd.tensor_tensor(new("num", u, 4), cvs[u // 2][:, cols_of(u)], held["pa", u][:], ALU.mult)
+
+        def denominator(u):
+            cv_sq, pa_sq = held["cv_sq", u], held["pa_sq", u]
+            if u >= turned_units:
+                nc.vector.tensor_tensor(new("den", u), cv_sq[:], pa_sq[:], ALU.add)
+                return
+            held["den", u] = psum.tile([P, BANK], F32, name="den_turned", bufs=2)
+            for block in blocks:
+                for first, term in ((True, cv_sq), (False, pa_sq)):
+                    nc.tensor.matmul(
+                        held["den", u][:, block], term[:, block], ident[:], is_transpose=True, start=first, stop=not first
+                    )
+
+        def root(u):
+            nc.scalar.activation(new("root", u, 3), held["den", u][:], ACT.Abs_reciprocal_sqrt, bias=0.5)
+
+        def twice(u):
+            return u < turned_units and u % 2 == 0
+
+        def inverse(u):
+            if twice(u):
+                factor = held["root", u]
+            else:
+                factor = new("inv", u)
+                nc.scalar.activation(factor, held["root", u][:], ACT.Square)
+            if u < turned_units:
+                back = psum.tile([P, BANK], F32, name="factor_back", bufs=2)
+                for block in blocks:
+                    nc.tensor.transpose(back[:, block], factor[:, block], ident[:])
+                factor = back
+            held["factor", u] = factor
 
         def finish(u):
+            factor, num = held["factor", u][:], held["num", u][:]
+            if twice(u):
+                half = new("half", u)
+                nc.vector.tensor_tensor(half, factor, num, ALU.mult)
+                num = half
             res = new("res", u, 3)
-            if u < shared:
-                nc.vector.scalar_tensor_tensor(res, held["bank", u][:], 0.125, held["ratio", u][:], ALU.mult, ALU.mult)
-            else:
-                nc.vector.tensor_tensor(res, held["num", u][:], held["inv", u][:], ALU.mult)
-            nc.sync.dma_start(out_rows[u // 2][:, cols_of(u)], res)
+            nc.vector.scalar_tensor_tensor(res, factor, 2.0, num, ALU.mult, ALU.mult)
+            nc.sync.dma_start(out_rows[u // 2][:, :, cols_of(u)], res)
 
         stages = (
-            (fetch, 1), (denominator, 0), (inverse, -1), (moments, 3), (square_cv, 1), (square_pa, 1), (ratio, -1),
-            (root, 0), (numerator, 0), (finish, -2),
+            (fetch, 2), (denominator, 0), (inverse, -1), (moments, 4), (square_cv, 2), (square_pa, 2), (numerator, 2),
+            (root, 0), (finish, -1),
         )
-        for step in range(-3, units + 2):
+        for step in range(-4, units + 1):
             for stage, ahead in stages:
                 if 0 <= step + ahead < units:
                     stage(step + ahead)

from contextlib import ExitStack

import concourse.mybir as mybir
from concourse.masks import make_identity

K, T, S, H, N, U = 512, 2048, 512, 512, 512, 1024
FLOPS = 2 * K * S * H + 2 * K * S * N + 2 * S * H * U

F32 = mybir.dt.float32
BF16 = mybir.dt.bfloat16
I32 = mybir.dt.int32
U32 = mybir.dt.uint32
U16 = mybir.dt.uint16
U8 = mybir.dt.uint8
FP8X4 = mybir.dt.float8_e4m3fn_x4
ALU = mybir.AluOpType
ACT = mybir.ActivationFunctionType

P = 128
PACK = 4
BANK = 512


def tile_picked_mombquadpagezharm_none_p_kernel(
    tc, x_words, x_scales, wa, wb, gt, gi, offs, two, n1, n2, n3, n4, n5, out
):
    nc = tc.nc
    with ExitStack() as ctx:
        keep = ctx.enter_context(tc.tile_pool(name="keep", bufs=1))
        ring = ctx.enter_context(tc.tile_pool(name="ring", bufs=3))
        psum = ctx.enter_context(tc.psum_pool(name="psum", bufs=4))

        def load_list(src, name):
            tile = keep.tile(list(src.shape), U16, name=name)
            nc.sync.dma_start(tile[:], src)
            return tile

        def load_weight(w, name, h):
            raw = keep.tile([P, PACK, 256], F32, name=f"{name}_raw{h}", tag=f"{name}_raw{h}")
            nc.sync.dma_start(raw[:], w[:, 256 * h : 256 * (h + 1)].rearrange("(p j) n -> p j n", j=PACK))
            return raw

        table_scales = keep.tile([P, T], U8, name="table_scales", align_bytes=64)
        nc.gpsimd.memset(table_scales[:].bitcast(I32), 0)
        two_l = load_list(two, "two_l")
        offs_l = load_list(offs, "offs_l")
        for q in range(4):
            nc.sync.dma_start(
                table_scales[32 * q : 32 * q + 4, :].bitcast(I32), x_scales[0, 4 * q : 4 * q + 4, :].bitcast(I32)
            )
        wb_raw = [load_weight(wb, "wb", h) for h in range(2)]
        gates_rows = keep.tile([P, P], F32, name="gates_rows")
        nc.vector.memset(gates_rows[:], 0.0)
        for row, g in ((0, gt), (PACK, gi)):
            nc.sync.dma_start(
                gates_rows[row : row + PACK, :].rearrange("t (g r) -> t g r", r=8),
                g.rearrange("(g t r) o -> t g (r o)", t=PACK, r=8),
            )
        table_words = keep.tile([P, T], I32, name="table_words", align_bytes=64)
        nc.sync.dma_start(table_words[:], x_words[0].rearrange("p c r -> p (c r)").bitcast(I32))
        n4_l = load_list(n4, "n4_l")
        n3_l = load_list(n3, "n3_l")
        wa_raw = [load_weight(wa, "wa", h) for h in range(2)]
        n1_l = load_list(n1, "n1_l")
        n2_l = load_list(n2, "n2_l")
        n5_l = load_list(n5, "n5_l")

        warm = keep.tile([P, 2], F32, name="warm")
        nc.vector.memset(warm[:, 0:1], 1.0)
        nc.scalar.activation(warm[:, 1:2], warm[:, 0:1], ACT.Abs_reciprocal_sqrt)

        ident = keep.tile([P, P], F32, name="ident")
        make_identity(nc, ident[:])
        gates_bank = psum.tile([P, BANK], F32, name="bank")
        nc.tensor.transpose(gates_bank[:, :P], gates_rows[:], ident[:])
        gt_c, gi_c = gates_bank[:, :PACK], gates_bank[:, PACK : 2 * PACK]
        half_sign = keep.tile([P, PACK], F32, name="half_sign")
        nc.vector.tensor_scalar(half_sign[:], gi_c, 0.0, 0.5, ALU.is_lt, ALU.subtract)
        gi_mag = keep.tile([P, PACK], F32, name="gi_mag")
        gi_neg = keep.tile([P, PACK], F32, name="gi_neg")
        a_scale = keep.tile([P, PACK], F32, name="a_scale")
        for dst, factor, gate in ((gi_mag, -2.0, gi_c), (gi_neg, 2.0, gi_c), (a_scale, 1.5, gt_c)):
            nc.vector.scalar_tensor_tensor(dst[:], half_sign[:], factor, gate, ALU.mult, ALU.mult)

        pages = [keep.tile([P, U], F32, name=f"page{t}") for t in range(PACK)]
        for page in pages:
            nc.gpsimd.memset(page[:], 0.0)

        def pick_words(lst, name):
            words = keep.tile([P, S], U32, name=f"{name}_words", align_bytes=64)
            nc.vector.tensor_copy(
                words[:].rearrange("p (t g r) -> p g t r", t=PACK, r=8), table_words[:].bitcast(U32).indirect(lst[:])
            )
            return words

        def pick_scales(lst, name):
            picked = keep.tile([P, S], U8, name=f"{name}_picked", align_bytes=64)
            nc.vector.tensor_copy(picked[:], table_scales[:].indirect(lst[:]))
            scales = keep.tile([P, S], U8, name=f"{name}_scales", align_bytes=64)
            nc.vector.tensor_copy(
                scales[:].bitcast(I32).rearrange("p (t g r) -> p g t r", t=PACK, r=2),
                picked[:].bitcast(I32).rearrange("p (g t r) -> p g t r", t=PACK, r=2),
            )
            return scales

        def interleave(dst, src):
            nc.scalar.copy(
                dst.rearrange("p (c i) t -> p c t i", i=4),
                src.rearrange("p t (c i) -> p c t i", i=4),
            )

        def quantize_weight(halves, name):
            grouped = keep.tile([P, BANK, PACK], BF16, name=f"{name}_grouped", tag=f"{name}_grouped", align_bytes=64)
            codes = keep.tile([P, BANK], U32, name=f"{name}_codes", align_bytes=64)
            scales = keep.tile([P, BANK], U8, name=f"{name}_plane", align_bytes=64)
            for h, raw in enumerate(halves):
                cols = slice(256 * h, 256 * (h + 1))
                interleave(grouped[:, cols, :], raw[:])
                nc.vector.quantize_mx(
                    codes[:, cols].bitcast(FP8X4), scales[:, cols], grouped[:, cols, :].rearrange("p n j -> p (n j)")
                )
            return codes, scales

        def product(lhs, t, rhs, cols):
            bank = psum.tile([P, BANK], F32, name="bank")
            rows = slice(P * t, P * (t + 1))
            nc.tensor.matmul_mx(
                bank[:],
                lhsT=lhs[0][:, rows].bitcast(FP8X4),
                lhsT_scale=lhs[1][:, rows],
                rhs=rhs[0][:, cols].bitcast(FP8X4),
                rhs_scale=rhs[1][:, cols],
                start=True,
                stop=True,
            )
            return bank

        scales_b = pick_scales(two_l, "b")
        scales_a = pick_scales(offs_l, "a")
        wb_q = quantize_weight(wb_raw, "wb")
        tokens_b = (pick_words(two_l, "b"), scales_b)
        tokens_a = (pick_words(offs_l, "a"), scales_a)

        b_rows = []
        for t in range(PACK):
            bank = product(tokens_b, t, wb_q, slice(0, N))
            rows = keep.tile([P, 2 * N], F32, name=f"b_rows{t}")
            neg = keep.tile([P, N], F32, name=f"b_neg{t}")
            nc.scalar.activation(rows[:, :N], bank[:], ACT.Relu, scale=gi_mag[:, t : t + 1])
            nc.scalar.activation(neg[:], bank[:], ACT.Copy, scale=gi_neg[:, t : t + 1])
            b_rows.append((rows, neg))

        wa_q = quantize_weight(wa_raw, "wa")
        a_rows = []
        for t in range(PACK):
            bank = product(tokens_a, t, wa_q, slice(0, H))
            first = keep.tile([P, 2 * H], F32, name=f"a_first{t}")
            second = keep.tile([P, 2 * H], F32, name=f"a_second{t}")
            nc.scalar.copy(first[:, :H], bank[:])
            nc.scalar.activation(second[:, :H], bank[:], ACT.Copy, scale=a_scale[:, t : t + 1])
            nc.scalar.activation(first[:, H:], bank[:], ACT.Copy, scale=a_scale[:, t : t + 1])
            a_rows.append((first, second))

        z2_planes = keep.tile([P, PACK, U], BF16, name="z2_planes", tag="wa_raw1")
        early = keep.tile([P, 2, N], F32, name="b_fetched_early")
        late = keep.tile([P, 2, N], F32, name="b_fetched_late", tag="wa_grouped", align_bytes=64)
        fetched = [early[:, 0, :], early[:, 1, :], late[:, 0, :], late[:, 1, :]]
        for t in range(PACK + 1):
            if t < PACK:
                nc.vector.tensor_copy(fetched[t], b_rows[t][0][:].indirect(n4_l[:]))
            if t > 0:
                s = t - 1
                nc.vector.tensor_tensor(pages[s][:].indirect(n3_l[:]), fetched[s], b_rows[s][1][:], ALU.add)
                nc.scalar.copy(z2_planes[:, s, :], pages[s][:])

        z2_grouped = keep.tile([P, U, PACK], BF16, name="z2_grouped", align_bytes=64)
        z2_codes = keep.tile([P, U], U32, name="z2_codes", align_bytes=64)
        z2_scales = keep.tile([P, U], U8, name="z2_scales", align_bytes=64)
        for h in range(2):
            cols = slice(BANK * h, BANK * (h + 1))
            interleave(z2_grouped[:, cols, :], z2_planes[:, :, cols])

        diffs = keep.tile([P, PACK, 2 * H], F32, name="diffs")
        for t in range(PACK):
            first, second = a_rows[t]
            got = ring.tile([P, 2 * H], F32, name="a_fetched", bufs=3)
            nc.vector.tensor_copy(got[:, :H], first[:].indirect(n1_l[:]))
            nc.vector.tensor_copy(got[:, H:], second[:].indirect(n2_l[:]))
            if t < PACK - 1:
                nc.gpsimd.tensor_tensor(diffs[:, t, :], got[:], first[:], ALU.subtract)
            else:
                for h in range(2):
                    cols = slice(BANK * h, BANK * (h + 1))
                    nc.vector.quantize_mx(
                        z2_codes[:, cols].bitcast(FP8X4),
                        z2_scales[:, cols],
                        z2_grouped[:, cols, :].rearrange("p n j -> p (n j)"),
                    )
                nc.vector.tensor_tensor(diffs[:, t, :], got[:], first[:], ALU.subtract)
        z_grouped = keep.tile([P, PACK, P, PACK], BF16, name="z_grouped", align_bytes=64)
        z_codes = keep.tile([P, H], U32, name="z_codes", align_bytes=64)
        z_scales = keep.tile([P, H], U8, name="z_scales", align_bytes=64)
        d1 = diffs[:, :, :H].rearrange("p t (a f i) -> p f a t i", f=PACK, i=4)
        d2 = diffs[:, :, H:].rearrange("p t (a f i) -> p f a t i", f=PACK, i=4)
        for f in range(PACK + 1):
            if f < PACK:
                nc.vector.tensor_tensor(
                    z_grouped[:, f].rearrange("p (a i) t -> p a t i", i=4), d1[:, f], d2[:, f], ALU.mult
                )
            if f > 0:
                rows = slice(P * (f - 1), P * f)
                nc.vector.quantize_mx(
                    z_codes[:, rows].bitcast(FP8X4), z_scales[:, rows], z_grouped[:, f - 1].rearrange("p m t -> p (m t)")
                )

        out_rows = out.rearrange("(a f i) w -> f a i w", f=PACK, i=4)
        units = 2 * PACK
        cvs = [keep.tile([P, U], F32, name=f"cv{f}", tag=f"b_rows{f}") for f in range(PACK)]
        held = {}
        turned_units = units - 2
        blocks = [slice(P * j, P * (j + 1)) for j in range(BANK // P)]

        def cols_of(u):
            return slice(BANK * (u % 2), BANK * (u % 2 + 1))

        def new(name, u, bufs=2):
            held[name, u] = ring.tile([P, BANK], F32, name=name, bufs=bufs)
            return held[name, u][:]

        def moments(u):
            bank = product((z_codes, z_scales), u // 2, (z2_codes, z2_scales), cols_of(u))
            cv = cvs[u // 2]
            if u == 1:
                nc.vector.tensor_scalar(cv[:, cols_of(u)], bank[:], 0.0625, None, ALU.mult)
            else:
                nc.scalar.activation(cv[:, cols_of(u)], bank[:], ACT.Copy, scale=0.0625)
            if u in (3, 5):
                both = ring.tile([P, U], F32, name="cv_sq_row", bufs=2)
                nc.gpsimd.tensor_tensor(both[:], cv[:], cv[:], ALU.mult)
                held["cv_sq", u - 1], held["cv_sq", u] = both[:, :BANK], both[:, BANK:]

        def fetch(u):
            nc.vector.tensor_copy(new("pa", u, 4), cvs[u // 2][:].indirect(n5_l[:, 32 * (u % 2) : 32 * (u % 2 + 1)]))

        def square_cv(u):
            if ("cv_sq", u) not in held:
                nc.scalar.activation(new("cv_sq", u), cvs[u // 2][:, cols_of(u)], ACT.Square)

        def square_pa(u):
            nc.scalar.activation(new("pa_sq", u, 3), held["pa", u][:], ACT.Square)

        def numerator(u):
            nc.gpsimd.tensor_tensor(new("num", u, 4), cvs[u // 2][:, cols_of(u)], held["pa", u][:], ALU.mult)

        def denominator(u):
            cv_sq, pa_sq = held["cv_sq", u], held["pa_sq", u]
            if u >= turned_units:
                nc.vector.tensor_tensor(new("den", u), cv_sq[:], pa_sq[:], ALU.add)
                return
            held["den", u] = psum.tile([P, BANK], F32, name="den_turned", bufs=2)
            for block in blocks:
                for first, term in ((True, cv_sq), (False, pa_sq)):
                    nc.tensor.matmul(
                        held["den", u][:, block], term[:, block], ident[:], is_transpose=True, start=first, stop=not first
                    )

        def root(u):
            nc.scalar.activation(new("root", u, 3), held["den", u][:], ACT.Abs_reciprocal_sqrt, bias=0.5)

        def twice(u):
            return u < turned_units and u % 2 == 0

        def inverse(u):
            if twice(u):
                factor = held["root", u]
            else:
                factor = new("inv", u)
                nc.scalar.activation(factor, held["root", u][:], ACT.Square)
            if u < turned_units:
                back = psum.tile([P, BANK], F32, name="factor_back", bufs=2)
                for block in blocks:
                    nc.tensor.transpose(back[:, block], factor[:, block], ident[:])
                factor = back
            held["factor", u] = factor

        def finish(u):
            factor, num = held["factor", u][:], held["num", u][:]
            if twice(u):
                half = new("half", u)
                nc.vector.tensor_tensor(half, factor, num, ALU.mult)
                num = half
            res = new("res", u, 3)
            nc.vector.scalar_tensor_tensor(res, factor, 2.0, num, ALU.mult, ALU.mult)
            nc.sync.dma_start(out_rows[u // 2][:, :, cols_of(u)], res)

        stages = (
            (fetch, 2), (denominator, 0), (inverse, -1), (moments, 4), (square_cv, 2), (square_pa, 2), (numerator, 2),
            (root, 0), (finish, -1),
        )
        for step in range(-4, units + 1):
            for stage, ahead in stages:
                if 0 <= step + ahead < units:
                    stage(step + ahead)
